import numpy as np
import ml_dtypes


def mxq(x, axis, fmt="e4m3"):
    dtype, down = {"e4m3": (ml_dtypes.float8_e4m3fn, 7), "e5m2": (ml_dtypes.float8_e5m2, 14)}[fmt]
    v = np.moveaxis(np.asarray(x, np.float32).astype(ml_dtypes.bfloat16).astype(np.float64), axis, -1)
    blocks = v.reshape(v.shape[:-1] + (-1, 32))
    amax = np.abs(blocks).max(-1, keepdims=True)
    byte = np.maximum(np.where(amax > 0, np.frexp(amax)[1] - 1 + 127, 0) - down, 1)
    scale = np.exp2(byte - 127.0)
    codes = (blocks / scale).astype(np.float32).astype(dtype).astype(np.float64)
    return np.moveaxis((codes * scale).reshape(v.shape), -1, axis)


WIDE = False


def mx_kscale(k):
    if not WIDE:
        return np.ones(k)
    levels = np.array([10, -10, 5, -5, 0])
    if k % 512:
        return np.exp2(np.random.permutation(np.resize(levels, k // 32))).repeat(32)
    a = np.empty((k // 512, 16))
    for p in range(k // 512):
        a[p, :8] = np.random.permutation(np.resize(levels, 8))
        for g in range(8):
            far = levels[np.abs(levels - a[p, g]) >= 10]
            a[p, g + 8] = far[np.random.randint(len(far))]
    return np.exp2(a.ravel()).repeat(32)


def f64(x):
    return np.asarray(x).astype(np.float64)


def striped(idx):
    return np.tile(np.asarray(idx).reshape(-1, 16).T, (8, 1)).astype(np.uint16)


def unstriped(offs):
    return offs[:16].T.reshape(-1).astype(np.int64)


E2M1 = np.array([0.0, 0.5, 1.0, 1.5, 2.0, 3.0, 4.0, 6.0, -0.0, -0.5, -1.0, -1.5, -2.0, -3.0, -4.0, -6.0])


def pack_weight(w, fmt):
    k, n = w.shape
    w = f64(np.asarray(w, np.float32).astype(ml_dtypes.bfloat16)).reshape(k // 32, 32, n)
    amax = np.abs(w).max(1)
    if fmt == "e4m3":
        byte = np.frexp(amax)[1] - 1 + 127 - 7
    else:
        mant, ex = np.frexp(amax / 6.0)
        byte = np.where(mant > 0.5, ex, ex - 1) + 127
    byte = np.clip(np.where(amax > 0, byte, 1), 1, 254)
    scaled = (w * np.exp2(127.0 - byte)[:, None, :]).reshape(k, n).astype(np.float32)
    by_word = np.ascontiguousarray(scaled.reshape(k // 512, 128, 4, n).transpose(0, 1, 3, 2))
    if fmt == "e4m3":
        words = by_word.astype(ml_dtypes.float8_e4m3fn).view(np.uint8)
    else:
        c = by_word.astype(ml_dtypes.float4_e2m1fn).view(np.uint8) & 0xF
        words = (c[..., 0::2] | (c[..., 1::2] << 4)).reshape(k // 512, 128, 2 * n)
    return np.ascontiguousarray(words), np.ascontiguousarray(byte.astype(np.uint8).reshape(k // 512, 16, n))


def unpack_weight(words, scales, fmt):
    g, _, n = scales.shape
    words = np.ascontiguousarray(words).reshape(g, 128, n, -1)
    if fmt == "e4m3":
        vals = words.view(ml_dtypes.float8_e4m3fn).astype(np.float64)
    else:
        nib = np.empty((g, 128, n, 4), np.uint8)
        nib[..., 0::2] = words & 0xF
        nib[..., 1::2] = words >> 4
        vals = E2M1[nib]
    vals = vals * np.repeat(np.exp2(scales.astype(np.float64) - 127.0), 8, axis=1)[..., None]
    return vals.transpose(0, 1, 3, 2).reshape(g * 512, n)


K, R, F, T, J, G = 512, 128, 512, 2048, 512, 64


def setup_inputs():
    n = np.random.standard_normal
    idx = np.random.permutation(T)[:J]
    fk = mx_kscale(K)
    ff = mx_kscale(F)
    tabp = pack_weight(n((K, T)) / fk[:, None], "e2m1")
    dtabp = pack_weight(n((K, T)) / fk[:, None], "e2m1")
    return {
        "tab_words": tabp[0],
        "tab_scales": tabp[1],
        "w1": (n((K, R)) * 1 / np.sqrt(K) * fk[:, None]).astype(np.float32),
        "share": (np.random.uniform(0.3, 1.2, (R, 1))).astype(np.float32),
        "wo": (n((F, R)) * 1 / np.sqrt(F) * ff[:, None]).astype(np.float32),
        "dy": (n((F, G)) / ff[:, None]).astype(np.float32),
        "dtab_words": dtabp[0],
        "dtab_scales": dtabp[1],
        "og": (np.random.uniform(0.7, 2.0, (R, 1))).astype(np.float32),
        "base": (0.3 * n((R, J))).astype(np.float32),
        "offs": striped(idx),
    }


def reference(tab_words, tab_scales, w1, share, wo, dy, dtab_words, dtab_scales, og, base, offs):
    idx = unstriped(offs)
    tabu = unpack_weight(tab_words, tab_scales, "e2m1")
    dtabu = unpack_weight(dtab_words, dtab_scales, "e2m1")
    w1q = mxq(f64(w1), 0, "e4m3")
    tabidxg = tabu[:, idx]
    a = w1q.T @ tabidxg
    dtabidxg = dtabu[:, idx]
    ta = w1q.T @ dtabidxg
    m1 = a.reshape(R, G, J // G).mean(axis=2)
    v1 = np.sqrt(np.square(a).reshape(R, G, J // G).mean(axis=2) - np.square(m1) + 0.05)
    u1 = np.tanh(v1 + m1 * f64(share))
    woq = mxq(f64(wo), 0, "e4m3")
    dyq = mxq(f64(dy), 0, "e4m3")
    c0 = woq.T @ dyq
    dv1 = c0 * (1.0 - np.square(u1))
    e1 = dv1 * 0.5 / np.sqrt(np.square(a).reshape(R, G, J // G).mean(axis=2) - np.square(m1) + 0.05) / 8.0
    r1 = np.repeat(e1, J // G, axis=1)
    xm1 = ta.reshape(R, G, J // G).mean(axis=2)
    xv1 = ((ta * a * 2.0).reshape(R, G, J // G).mean(axis=2) - xm1 * m1 * 2.0) * 0.5 / v1
    xu1 = (xv1 + xm1 * f64(share)) * (1.0 - np.square(u1))
    xdv1 = xu1 * u1 * 2.0 * (-1.0) * c0
    xe1 = (xdv1 * 0.5 - ((ta * a * 2.0).reshape(R, G, J // G).mean(axis=2) - xm1 * m1 * 2.0) * 0.5 / np.sqrt(np.square(a).reshape(R, G, J // G).mean(axis=2) - np.square(m1) + 0.05) * dv1 * 0.5 / np.sqrt(np.square(a).reshape(R, G, J // G).mean(axis=2) - np.square(m1) + 0.05)) / np.sqrt(np.square(a).reshape(R, G, J // G).mean(axis=2) - np.square(m1) + 0.05) / 8.0
    xr1 = np.repeat(xe1, J // G, axis=1)
    xdm1 = xu1 * u1 * 2.0 * (-1.0) * c0 * f64(share) + ((xdv1 * 0.5 - ((ta * a * 2.0).reshape(R, G, J // G).mean(axis=2) - xm1 * m1 * 2.0) * 0.5 / np.sqrt(np.square(a).reshape(R, G, J // G).mean(axis=2) - np.square(m1) + 0.05) * dv1 * 0.5 / np.sqrt(np.square(a).reshape(R, G, J // G).mean(axis=2) - np.square(m1) + 0.05)) / np.sqrt(np.square(a).reshape(R, G, J // G).mean(axis=2) - np.square(m1) + 0.05) * (-1.0) * m1 + xm1 * dv1 * 0.5 / np.sqrt(np.square(a).reshape(R, G, J // G).mean(axis=2) - np.square(m1) + 0.05) * (-1.0)) * 2.0
    xe2 = xdm1 / 8.0
    xr2 = np.repeat(xe2, J // G, axis=1)
    xda = (xr1 * a + ta * r1) * 2.0 + xr2
    y = xda * f64(og) + f64(base)
    return y

@@ -1,0 +1,186 @@
+from contextlib import ExitStack
+
+import concourse.mybir as mybir
+
+K, R, F, T, J, G = 512, 128, 512, 2048, 512, 64
+W = J // G
+P = 128
+FLOPS = 2 * K * R * J * 2 + 2 * F * R * G
+
+F32 = mybir.dt.float32
+BF16 = mybir.dt.bfloat16
+I32 = mybir.dt.int32
+U32 = mybir.dt.uint32
+U16 = mybir.dt.uint16
+U8 = mybir.dt.uint8
+FP8X4 = mybir.dt.float8_e4m3fn_x4
+FP4X4 = mybir.dt.float4_e2m1fn_x4
+ACT = mybir.ActivationFunctionType
+ALU = mybir.AluOpType
+AX = mybir.AxisListType
+
+
+def tile_attend_hvspreadpool_kernel(tc, tab_words, tab_scales, w1, share, wo, dy, dtab_words, dtab_scales, og, base, offs, out):
+    nc = tc.nc
+    mult, add, sub = ALU.mult, ALU.add, ALU.subtract
+    with ExitStack() as ctx:
+        sb = ctx.enter_context(tc.tile_pool(name="sb", bufs=1))
+        ps = ctx.enter_context(tc.psum_pool(name="ps", bufs=1))
+
+        def t32(name, shape, tag=None):
+            return sb.tile(shape, F32, name=name, tag=tag or name, align_bytes=64)
+
+        def grp(ap):
+            return ap.rearrange("p (g i) -> p g i", i=W)
+
+        def spread(ap):
+            return ap.unsqueeze(2).to_broadcast([P, ap.shape[1], W])
+
+        offsets = sb.tile([P, J // 16], U16, name="offsets")
+        tw = sb.tile([P, T], U16, name="tw", align_bytes=64)
+        dw = sb.tile([P, T], U16, name="dw", align_bytes=64)
+        ts = sb.tile([P, T], U8, name="ts", align_bytes=64)
+        ds = sb.tile([P, T], U8, name="ds", align_bytes=64)
+        w1r = t32("w1r", [P, 4, R])
+        wor = t32("wor", [P, 4, R])
+        dyr = t32("dyr", [P, 4, G])
+        bs = t32("bs", [P, J])
+        sh = t32("sh", [P, 1])
+        ogt = t32("ogt", [P, 1])
+        warm = t32("warm", [P, 1])
+        warm2 = t32("warm2", [P, 1])
+
+        nc.vector.memset(ts[:].bitcast(I32), 0)
+        nc.vector.memset(ds[:].bitcast(I32), 0)
+        nc.vector.memset(warm[:], 1.0)
+        nc.sync.dma_start(offsets[:], offs)
+        nc.sync.dma_start(w1r[:], w1.rearrange("(p t) r -> p t r", t=4))
+        nc.sync.dma_start(tw[:].bitcast(I32), tab_words[0].bitcast(I32))
+        for q in range(4):
+            nc.scalar.dma_start(ts[32 * q : 32 * q + 4, :].bitcast(I32), tab_scales[0, 4 * q : 4 * q + 4, :].bitcast(I32))
+        nc.sync.dma_start(dw[:].bitcast(I32), dtab_words[0].bitcast(I32))
+        for q in range(4):
+            nc.scalar.dma_start(ds[32 * q : 32 * q + 4, :].bitcast(I32), dtab_scales[0, 4 * q : 4 * q + 4, :].bitcast(I32))
+        nc.scalar.activation(warm2[:], warm[:], ACT.Abs_reciprocal_sqrt)
+        nc.sync.dma_start(wor[:], wo.rearrange("(p t) r -> p t r", t=4))
+        nc.sync.dma_start(dyr[:], dy.rearrange("(p t) g -> p t g", t=4))
+        nc.sync.dma_start(bs[:], base)
+        nc.gpsimd.dma_start(sh[:], share)
+        nc.gpsimd.dma_start(ogt[:], og)
+
+        con = t32("con", [P, 4])
+        s8, s2, ss2, og8 = con[:, 0:1], con[:, 1:2], con[:, 2:3], con[:, 3:4]
+        nc.gpsimd.tensor_scalar(s8, sh[:], 0.125, 0.0, mult, add)
+        nc.gpsimd.tensor_scalar(s2, sh[:], 2.0, 0.0, mult, add)
+        nc.gpsimd.tensor_scalar(ss2, sh[:], sh[:, 0:1], 2.0, mult, mult)
+        nc.gpsimd.tensor_scalar(og8, ogt[:], 0.125, 0.0, mult, add)
+
+        def quant(name, raw, width, cast):
+            grouped = sb.tile([P, width, 4], BF16, name=name + "_b", align_bytes=64)
+            codes = sb.tile([P, width], U32, name=name + "_c", align_bytes=64)
+            scales = sb.tile([P, width], U8, name=name + "_s", align_bytes=64)
+            cast(grouped[:], raw[:].rearrange("p t w -> p w t"))
+            nc.vector.quantize_mx(out=codes[:].bitcast(FP8X4), scales=scales[:], in_=grouped[:].rearrange("p w t -> p (w t)"))
+            return codes, scales
+
+        gtw = sb.tile([P, J], U16, name="gtw", align_bytes=64)
+        gts = sb.tile([P, J], U8, name="gts", align_bytes=64)
+        pa = ps.tile([P, J], F32, name="pa")
+        pt = [ps.tile([P, J // 2], F32, name="pt0"), ps.tile([P, J // 2], F32, name="pt1")]
+        pc = ps.tile([P, G], F32, name="pc")
+
+        w1c, w1s = quant("w1", w1r, R, nc.vector.tensor_copy)
+        nc.vector.tensor_copy(gts[:], ts[:].indirect(offsets[:]))
+        nc.vector.tensor_copy(gtw[:], tw[:].indirect(offsets[:]))
+        nc.tensor.matmul_mx(out=pa[:], lhsT=w1c[:].bitcast(FP8X4), lhsT_scale=w1s[:], rhs=gtw[:].bitcast(FP4X4), rhs_scale=gts[:], start=True, stop=True)
+        gdw = sb.tile([P, J], U16, name="gdw", tag="ts", align_bytes=64)
+        nc.vector.tensor_copy(gdw[:], dw[:].indirect(offsets[:]))
+
+        woc, wos = quant("wo", wor, R, nc.scalar.copy)
+        dyc, dys = quant("dy", dyr, G, nc.scalar.copy)
+        nc.tensor.matmul_mx(out=pc[:], lhsT=woc[:].bitcast(FP8X4), lhsT_scale=wos[:], rhs=dyc[:].bitcast(FP8X4), rhs_scale=dys[:], start=True, stop=True)
+        halves = [(slice(0, J // 2), slice(0, G // 2)), (slice(J // 2, J), slice(G // 2, G))]
+        sq = t32("sq", [P, J])
+        asb = t32("asb", [P, J])
+        s1 = t32("s1", [P, G])
+        s2t = t32("s2t", [P, G])
+        msq = t32("msq", [P, G])
+        var = t32("var", [P, G])
+        iv = t32("iv", [P, G])
+        nc.scalar.activation(sq[:], pa[:], ACT.Square)
+        nc.vector.tensor_reduce(s1[:], grp(pa[:]), AX.X, add)
+        nc.vector.tensor_reduce(s2t[:], grp(sq[:]), AX.X, add)
+        nc.scalar.activation(msq[:], s1[:], ACT.Square, scale=0.125)
+        nc.scalar.copy(asb[:], pa[:])
+        nc.vector.scalar_tensor_tensor(var[:], s2t[:], 0.125, msq[:], mult, sub)
+        nc.scalar.activation(iv[:], var[:], ACT.Abs_reciprocal_sqrt, bias=0.05)
+        warm3 = t32("warm3", [P, 1])
+        nc.scalar.activation(warm3[:], iv[:, 0:1], ACT.Tanh)
+        gds = sb.tile([P, J], U8, name="gds", tag="sq", align_bytes=64)
+        for h, (cols, gs) in enumerate(halves):
+            nc.vector.tensor_copy(gds[:, cols], ds[:].indirect(offsets[:, 16 * h : 16 * (h + 1)]))
+            nc.tensor.matmul_mx(out=pt[h][:], lhsT=w1c[:].bitcast(FP8X4), lhsT_scale=w1s[:], rhs=gdw[:, cols].bitcast(FP4X4), rhs_scale=gds[:, cols], start=True, stop=True)
+
+        v = t32("v", [P, G])
+        pre = t32("pre", [P, G])
+        gg = t32("gg", [P, G])
+        u = t32("u", [P, G])
+        u2 = t32("u2", [P, G])
+        nc.vector.scalar_tensor_tensor(v[:], var[:], 0.05, iv[:], add, mult)
+        nc.vector.scalar_tensor_tensor(gg[:], pc[:], og8, iv[:], mult, mult)
+        nc.vector.scalar_tensor_tensor(pre[:], s1[:], s8, v[:], mult, add)
+        nc.scalar.activation(u[:], pre[:], ACT.Tanh)
+        nc.scalar.activation(u2[:], u[:], ACT.Square)
+
+        pr = t32("pr", [P, J], tag="var")
+        t1 = t32("t1", [P, G])
+        cr = t32("cr", [P, G])
+        cv = t32("cv", [P, G])
+        mt = t32("mt", [P, G])
+        nb = t32("nb", [P, G])
+        x = t32("x", [P, G])
+        xi = t32("xi", [P, G])
+        y = t32("y", [P, G])
+        co = t32("co", [P, 3, G])
+        for h, (cols, gs) in enumerate(halves):
+            nc.vector.scalar_tensor_tensor(pr[:, cols], pt[h][:], 0.125, asb[:, cols], mult, mult)
+            nc.vector.tensor_reduce(t1[:, gs], grp(pt[h][:]), AX.X, add)
+        nc.vector.scalar_tensor_tensor(x[:], u[:], 2.0, iv[:], mult, add)
+        nc.vector.scalar_tensor_tensor(y[:], u[:], ss2, v[:], mult, mult)
+        nc.vector.scalar_tensor_tensor(nb[:], u2[:], 1.0, gg[:], sub, mult)
+        nc.vector.scalar_tensor_tensor(mt[:], s1[:], 1.0 / 64, t1[:], mult, mult)
+        nc.vector.tensor_tensor(xi[:], x[:], iv[:], mult)
+        nc.vector.tensor_reduce(cr[:], grp(pr[:]), AX.X, add)
+        nc.vector.scalar_tensor_tensor(co[:, 2, :], y[:], 1.0, nb[:], add, mult)
+        nc.vector.scalar_tensor_tensor(co[:, 1, :], u[:], s2, nb[:], mult, mult)
+        nc.vector.tensor_tensor(co[:, 0, :], xi[:], nb[:], mult)
+        nc.vector.tensor_tensor(cv[:], cr[:], mt[:], sub)
+
+        bta = t32("bta", [P, J])
+        yb = t32("yb", [P, J])
+        ad0 = t32("ad0", [P, 2, G])
+        ad1 = t32("ad1", [P, 2, G])
+        ad = t32("ad", [P, 2, G])
+        am = t32("am", [P, G])
+        cc = t32("cc", [P, G])
+        e1 = t32("e1", [P, J])
+        e2 = t32("e2", [P, J])
+        res = [t32("res0", [P, J // 2]), t32("res1", [P, J // 2])]
+        (c0, g0), (c1, g1) = halves
+        nc.vector.scalar_tensor_tensor(ad0[:], t1[:].unsqueeze(1).to_broadcast([P, 2, G]), 0.125, co[:, 1:3, :], mult, mult)
+        nc.vector.tensor_tensor(grp(bta[:, c0]), grp(pt[0][:]), spread(nb[:, g0]), mult)
+        nc.vector.tensor_tensor(ad1[:], cv[:].unsqueeze(1).to_broadcast([P, 2, G]), co[:, 0:2, :], mult)
+        nc.vector.tensor_tensor(grp(bta[:, c1]), grp(pt[1][:]), spread(nb[:, g1]), mult)
+        nc.vector.tensor_tensor(ad[:], ad0[:], ad1[:], add)
+        nc.vector.tensor_tensor(yb[:, c0], bs[:, c0], bta[:, c0], sub)
+        nc.vector.scalar_tensor_tensor(am[:], s1[:], 0.125, ad[:, 0, :], mult, mult)
+        nc.vector.tensor_tensor(grp(e1[:, c0]), grp(asb[:, c0]), spread(ad[:, 0, g0]), mult)
+        nc.vector.tensor_tensor(cc[:], ad[:, 1, :], am[:], sub)
+        nc.vector.tensor_tensor(yb[:, c1], bs[:, c1], bta[:, c1], sub)
+        nc.vector.tensor_tensor(grp(e2[:, c0]), grp(yb[:, c0]), spread(cc[:, g0]), add)
+        nc.vector.tensor_tensor(grp(e1[:, c1]), grp(asb[:, c1]), spread(ad[:, 0, g1]), mult)
+        nc.vector.tensor_tensor(res[0][:], e1[:, c0], e2[:, c0], add)
+        nc.sync.dma_start(out[:, c0], res[0][:])
+        nc.vector.tensor_tensor(grp(e2[:, c1]), grp(yb[:, c1]), spread(cc[:, g1]), add)
+        nc.vector.tensor_tensor(res[1][:], e1[:, c1], e2[:, c1], add)
+        nc.sync.dma_start(out[:, c1], res[1][:])

@@ -25,10 +25,14 @@ def tile_attend_hvspreadpool_kernel(tc, tab_words, tab_scales, w1, share, wo, dy
     mult, add, sub = ALU.mult, ALU.add, ALU.subtract
     with ExitStack() as ctx:
         sb = ctx.enter_context(tc.tile_pool(name="sb", bufs=1))
+        shared = ctx.enter_context(tc.tile_pool(name="shared", bufs=1))
         ps = ctx.enter_context(tc.psum_pool(name="ps", bufs=1))
 
         def t32(name, shape, tag=None):
             return sb.tile(shape, F32, name=name, tag=tag or name, align_bytes=64)
+
+        def at(offset, name, shape, dtype=F32):
+            return shared.tile(shape, dtype, name=name, offset=offset, align_bytes=64)
 
         def grp(ap):
             return ap.rearrange("p (g i) -> p g i", i=W)
@@ -40,7 +44,7 @@ def tile_attend_hvspreadpool_kernel(tc, tab_words, tab_scales, w1, share, wo, dy
         tw = sb.tile([P, T], U16, name="tw", align_bytes=64)
         dw = sb.tile([P, T], U16, name="dw", align_bytes=64)
         ts = sb.tile([P, T], U8, name="ts", align_bytes=64)
-        ds = sb.tile([P, T], U8, name="ds", align_bytes=64)
+        ds = at(960, "ds", [P, T], U8)
         w1r = t32("w1r", [P, 4, R])
         wor = t32("wor", [P, 4, R])
         dyr = t32("dyr", [P, 4, G])
@@ -52,16 +56,19 @@ def tile_attend_hvspreadpool_kernel(tc, tab_words, tab_scales, w1, share, wo, dy
 
         nc.vector.memset(ts[:].bitcast(I32), 0)
         nc.vector.memset(ds[:].bitcast(I32), 0)
-        nc.vector.memset(warm[:], 1.0)
-        nc.sync.dma_start(offsets[:], offs)
-        nc.sync.dma_start(w1r[:], w1.rearrange("(p t) r -> p t r", t=4))
-        nc.sync.dma_start(tw[:].bitcast(I32), tab_words[0].bitcast(I32))
-        for q in range(4):
-            nc.scalar.dma_start(ts[32 * q : 32 * q + 4, :].bitcast(I32), tab_scales[0, 4 * q : 4 * q + 4, :].bitcast(I32))
-        nc.sync.dma_start(dw[:].bitcast(I32), dtab_words[0].bitcast(I32))
-        for q in range(4):
-            nc.scalar.dma_start(ds[32 * q : 32 * q + 4, :].bitcast(I32), dtab_scales[0, 4 * q : 4 * q + 4, :].bitcast(I32))
+        nc.gpsimd.memset(warm[:], 1.0)
         nc.scalar.activation(warm2[:], warm[:], ACT.Abs_reciprocal_sqrt)
+        nc.sync.dma_start(offsets[:], offs)
+        def load_scales(tile, rows):
+            by_row = rows[0].rearrange("(q r) c -> r q c", r=4)
+            for r in range(4):
+                nc.sync.dma_start(tile[r:P:32, :].bitcast(I32), by_row[r].bitcast(I32))
+
+        nc.sync.dma_start(tw[:].bitcast(I32), tab_words[0].bitcast(I32))
+        load_scales(ts, tab_scales)
+        nc.sync.dma_start(w1r[:], w1.rearrange("(p t) r -> p t r", t=4))
+        nc.sync.dma_start(dw[:].bitcast(I32), dtab_words[0].bitcast(I32))
+        load_scales(ds, dtab_scales)
         nc.sync.dma_start(wor[:], wo.rearrange("(p t) r -> p t r", t=4))
         nc.sync.dma_start(dyr[:], dy.rearrange("(p t) g -> p t g", t=4))
         nc.sync.dma_start(bs[:], base)
@@ -75,51 +82,60 @@ def tile_attend_hvspreadpool_kernel(tc, tab_words, tab_scales, w1, share, wo, dy
         nc.gpsimd.tensor_scalar(ss2, sh[:], sh[:, 0:1], 2.0, mult, mult)
         nc.gpsimd.tensor_scalar(og8, ogt[:], 0.125, 0.0, mult, add)
 
-        def quant(name, raw, width, cast):
-            grouped = sb.tile([P, width, 4], BF16, name=name + "_b", align_bytes=64)
-            codes = sb.tile([P, width], U32, name=name + "_c", align_bytes=64)
-            scales = sb.tile([P, width], U8, name=name + "_s", align_bytes=64)
-            cast(grouped[:], raw[:].rearrange("p t w -> p w t"))
+        def cast(grouped, raw):
+            nc.scalar.copy(grouped[:], raw[:].rearrange("p t w -> p w t"))
+            return grouped
+
+        def quant(name, codes, grouped):
+            scales = sb.tile([P, codes.shape[1]], U8, name=name + "_s", align_bytes=64)
             nc.vector.quantize_mx(out=codes[:].bitcast(FP8X4), scales=scales[:], in_=grouped[:].rearrange("p w t -> p (w t)"))
             return codes, scales
 
+        halves = [(slice(0, J // 2), slice(0, G // 2)), (slice(J // 2, J), slice(G // 2, G))]
+        (c0, g0), (c1, g1) = halves
         gtw = sb.tile([P, J], U16, name="gtw", align_bytes=64)
         gts = sb.tile([P, J], U8, name="gts", align_bytes=64)
+        gds = sb.tile([P, J], U8, name="gds", align_bytes=64)
         pa = ps.tile([P, J], F32, name="pa")
         pt = [ps.tile([P, J // 2], F32, name="pt0"), ps.tile([P, J // 2], F32, name="pt1")]
         pc = ps.tile([P, G], F32, name="pc")
 
-        w1c, w1s = quant("w1", w1r, R, nc.vector.tensor_copy)
-        nc.vector.tensor_copy(gts[:], ts[:].indirect(offsets[:]))
         nc.vector.tensor_copy(gtw[:], tw[:].indirect(offsets[:]))
+        nc.vector.tensor_copy(gts[:], ts[:].indirect(offsets[:]))
+        w1c, w1s = quant("w1", sb.tile([P, R], U32, name="w1c", align_bytes=64), cast(sb.tile([P, R, 4], BF16, name="w1_b", align_bytes=64), w1r))
         nc.tensor.matmul_mx(out=pa[:], lhsT=w1c[:].bitcast(FP8X4), lhsT_scale=w1s[:], rhs=gtw[:].bitcast(FP4X4), rhs_scale=gts[:], start=True, stop=True)
-        gdw = sb.tile([P, J], U16, name="gdw", tag="ts", align_bytes=64)
-        nc.vector.tensor_copy(gdw[:], dw[:].indirect(offsets[:]))
 
-        woc, wos = quant("wo", wor, R, nc.scalar.copy)
-        dyc, dys = quant("dy", dyr, G, nc.scalar.copy)
-        nc.tensor.matmul_mx(out=pc[:], lhsT=woc[:].bitcast(FP8X4), lhsT_scale=wos[:], rhs=dyc[:].bitcast(FP8X4), rhs_scale=dys[:], start=True, stop=True)
-        halves = [(slice(0, J // 2), slice(0, G // 2)), (slice(J // 2, J), slice(G // 2, G))]
+        def direction_half(h, words):
+            nc.vector.tensor_copy(words[:], dw[:].indirect(offsets[:, 16 * h : 16 * (h + 1)]))
+            return words
+
+        def direction_product(h, words):
+            nc.tensor.matmul_mx(out=pt[h][:], lhsT=w1c[:].bitcast(FP8X4), lhsT_scale=w1s[:], rhs=words[:].bitcast(FP4X4), rhs_scale=gds[:, halves[h][0]], start=True, stop=True)
+
+        gdw0 = direction_half(0, sb.tile([P, J // 2], U16, name="gdw0", tag="w1_b", align_bytes=64))
+        nc.vector.tensor_copy(gds[:], ds[:].indirect(offsets[:]))
+        direction_product(0, gdw0)
+
         sq = t32("sq", [P, J])
         asb = t32("asb", [P, J])
-        s1 = t32("s1", [P, G])
-        s2t = t32("s2t", [P, G])
-        msq = t32("msq", [P, G])
+        s1 = at(1024, "s1", [P, G])
+        s2t = at(1280, "s2t", [P, G])
+        msq = at(1536, "msq", [P, G])
         var = t32("var", [P, G])
         iv = t32("iv", [P, G])
-        nc.scalar.activation(sq[:], pa[:], ACT.Square)
-        nc.vector.tensor_reduce(s1[:], grp(pa[:]), AX.X, add)
-        nc.vector.tensor_reduce(s2t[:], grp(sq[:]), AX.X, add)
-        nc.scalar.activation(msq[:], s1[:], ACT.Square, scale=0.125)
         nc.scalar.copy(asb[:], pa[:])
+        nc.scalar.activation(sq[:], pa[:], ACT.Square)
+        nc.vector.tensor_reduce(s1[:], grp(asb[:]), AX.X, add)
+        nc.vector.tensor_reduce(s2t[:], grp(sq[:]), AX.X, add)
+        nc.vector.scalar_tensor_tensor(msq[:], s1[:], 1.0 / 64, s1[:], mult, mult)
+        wob = cast(at(0, "wob", [P, R, 4], BF16), wor)
+        dyb = cast(at(2560, "dyb", [P, G, 4], BF16), dyr)
+        woc, wos = quant("wo", at(1792, "woc", [P, R], U32), wob)
         nc.vector.scalar_tensor_tensor(var[:], s2t[:], 0.125, msq[:], mult, sub)
         nc.scalar.activation(iv[:], var[:], ACT.Abs_reciprocal_sqrt, bias=0.05)
-        warm3 = t32("warm3", [P, 1])
-        nc.scalar.activation(warm3[:], iv[:, 0:1], ACT.Tanh)
-        gds = sb.tile([P, J], U8, name="gds", tag="sq", align_bytes=64)
-        for h, (cols, gs) in enumerate(halves):
-            nc.vector.tensor_copy(gds[:, cols], ds[:].indirect(offsets[:, 16 * h : 16 * (h + 1)]))
-            nc.tensor.matmul_mx(out=pt[h][:], lhsT=w1c[:].bitcast(FP8X4), lhsT_scale=w1s[:], rhs=gdw[:, cols].bitcast(FP4X4), rhs_scale=gds[:, cols], start=True, stop=True)
+        dyc, dys = quant("dy", at(2304, "dyc", [P, G], U32), dyb)
+        direction_product(1, direction_half(1, at(1280, "gdw1", [P, J // 2], U16)))
+        nc.tensor.matmul_mx(out=pc[:], lhsT=woc[:].bitcast(FP8X4), lhsT_scale=wos[:], rhs=dyc[:].bitcast(FP8X4), rhs_scale=dys[:], start=True, stop=True)
 
         v = t32("v", [P, G])
         pre = t32("pre", [P, G])
@@ -127,13 +143,12 @@ def tile_attend_hvspreadpool_kernel(tc, tab_words, tab_scales, w1, share, wo, dy
         u = t32("u", [P, G])
         u2 = t32("u2", [P, G])
         nc.vector.scalar_tensor_tensor(v[:], var[:], 0.05, iv[:], add, mult)
-        nc.vector.scalar_tensor_tensor(gg[:], pc[:], og8, iv[:], mult, mult)
         nc.vector.scalar_tensor_tensor(pre[:], s1[:], s8, v[:], mult, add)
         nc.scalar.activation(u[:], pre[:], ACT.Tanh)
         nc.scalar.activation(u2[:], u[:], ACT.Square)
 
-        pr = t32("pr", [P, J], tag="var")
-        t1 = t32("t1", [P, G])
+        prt = t32("prt", [P, J + G], tag="var")
+        pr, t1 = prt[:, 0:J], prt[:, J : J + G]
         cr = t32("cr", [P, G])
         cv = t32("cv", [P, G])
         mt = t32("mt", [P, G])
@@ -145,12 +160,13 @@ def tile_attend_hvspreadpool_kernel(tc, tab_words, tab_scales, w1, share, wo, dy
         for h, (cols, gs) in enumerate(halves):
             nc.vector.scalar_tensor_tensor(pr[:, cols], pt[h][:], 0.125, asb[:, cols], mult, mult)
             nc.vector.tensor_reduce(t1[:, gs], grp(pt[h][:]), AX.X, add)
+        nc.vector.scalar_tensor_tensor(gg[:], pc[:], og8, iv[:], mult, mult)
         nc.vector.scalar_tensor_tensor(x[:], u[:], 2.0, iv[:], mult, add)
         nc.vector.scalar_tensor_tensor(y[:], u[:], ss2, v[:], mult, mult)
         nc.vector.scalar_tensor_tensor(nb[:], u2[:], 1.0, gg[:], sub, mult)
-        nc.vector.scalar_tensor_tensor(mt[:], s1[:], 1.0 / 64, t1[:], mult, mult)
+        nc.vector.scalar_tensor_tensor(mt[:], s1[:], 1.0 / 64, t1, mult, mult)
         nc.vector.tensor_tensor(xi[:], x[:], iv[:], mult)
-        nc.vector.tensor_reduce(cr[:], grp(pr[:]), AX.X, add)
+        nc.vector.tensor_reduce(cr[:], grp(pr), AX.X, add)
         nc.vector.scalar_tensor_tensor(co[:, 2, :], y[:], 1.0, nb[:], add, mult)
         nc.vector.scalar_tensor_tensor(co[:, 1, :], u[:], s2, nb[:], mult, mult)
         nc.vector.tensor_tensor(co[:, 0, :], xi[:], nb[:], mult)
@@ -166,8 +182,7 @@ def tile_attend_hvspreadpool_kernel(tc, tab_words, tab_scales, w1, share, wo, dy
         e1 = t32("e1", [P, J])
         e2 = t32("e2", [P, J])
         res = [t32("res0", [P, J // 2]), t32("res1", [P, J // 2])]
-        (c0, g0), (c1, g1) = halves
-        nc.vector.scalar_tensor_tensor(ad0[:], t1[:].unsqueeze(1).to_broadcast([P, 2, G]), 0.125, co[:, 1:3, :], mult, mult)
+        nc.vector.scalar_tensor_tensor(ad0[:], t1.unsqueeze(1).to_broadcast([P, 2, G]), 0.125, co[:, 1:3, :], mult, mult)
         nc.vector.tensor_tensor(grp(bta[:, c0]), grp(pt[0][:]), spread(nb[:, g0]), mult)
         nc.vector.tensor_tensor(ad1[:], cv[:].unsqueeze(1).to_broadcast([P, 2, G]), co[:, 0:2, :], mult)
         nc.vector.tensor_tensor(grp(bta[:, c1]), grp(pt[1][:]), spread(nb[:, g1]), mult)
@@ -179,8 +194,8 @@ def tile_attend_hvspreadpool_kernel(tc, tab_words, tab_scales, w1, share, wo, dy
         nc.vector.tensor_tensor(yb[:, c1], bs[:, c1], bta[:, c1], sub)
         nc.vector.tensor_tensor(grp(e2[:, c0]), grp(yb[:, c0]), spread(cc[:, g0]), add)
         nc.vector.tensor_tensor(grp(e1[:, c1]), grp(asb[:, c1]), spread(ad[:, 0, g1]), mult)
+        nc.vector.tensor_tensor(grp(e2[:, c1]), grp(yb[:, c1]), spread(cc[:, g1]), add)
         nc.vector.tensor_tensor(res[0][:], e1[:, c0], e2[:, c0], add)
         nc.sync.dma_start(out[:, c0], res[0][:])
-        nc.vector.tensor_tensor(grp(e2[:, c1]), grp(yb[:, c1]), spread(cc[:, g1]), add)
         nc.vector.tensor_tensor(res[1][:], e1[:, c1], e2[:, c1], add)
         nc.sync.dma_start(out[:, c1], res[1][:])

@@ -43,9 +43,9 @@ def tile_attend_hvspreadpool_kernel(tc, tab_words, tab_scales, w1, share, wo, dy
         offsets = sb.tile([P, J // 16], U16, name="offsets")
         tw = sb.tile([P, T], U16, name="tw", align_bytes=64)
         dw = sb.tile([P, T], U16, name="dw", align_bytes=64)
-        ts = sb.tile([P, T], U8, name="ts", align_bytes=64)
+        ts = at(5120, "ts", [P, T], U8)
         ds = at(960, "ds", [P, T], U8)
-        w1r = t32("w1r", [P, 4, R])
+        w1r = at(3072, "w1r", [P, 4, R])
         wor = t32("wor", [P, 4, R])
         dyr = t32("dyr", [P, 4, G])
         bs = t32("bs", [P, J])
@@ -57,6 +57,8 @@ def tile_attend_hvspreadpool_kernel(tc, tab_words, tab_scales, w1, share, wo, dy
         nc.vector.memset(ts[:].bitcast(I32), 0)
         nc.vector.memset(ds[:].bitcast(I32), 0)
         nc.gpsimd.memset(warm[:], 1.0)
+        nc.scalar.dma_start(sh[:], share)
+        nc.scalar.dma_start(ogt[:], og)
         nc.scalar.activation(warm2[:], warm[:], ACT.Abs_reciprocal_sqrt)
         nc.sync.dma_start(offsets[:], offs)
         def load_scales(tile, rows):
@@ -72,15 +74,13 @@ def tile_attend_hvspreadpool_kernel(tc, tab_words, tab_scales, w1, share, wo, dy
         nc.sync.dma_start(wor[:], wo.rearrange("(p t) r -> p t r", t=4))
         nc.sync.dma_start(dyr[:], dy.rearrange("(p t) g -> p t g", t=4))
         nc.sync.dma_start(bs[:], base)
-        nc.gpsimd.dma_start(sh[:], share)
-        nc.gpsimd.dma_start(ogt[:], og)
 
         con = t32("con", [P, 4])
         s8, s2, ss2, og8 = con[:, 0:1], con[:, 1:2], con[:, 2:3], con[:, 3:4]
-        nc.gpsimd.tensor_scalar(s8, sh[:], 0.125, 0.0, mult, add)
-        nc.gpsimd.tensor_scalar(s2, sh[:], 2.0, 0.0, mult, add)
-        nc.gpsimd.tensor_scalar(ss2, sh[:], sh[:, 0:1], 2.0, mult, mult)
-        nc.gpsimd.tensor_scalar(og8, ogt[:], 0.125, 0.0, mult, add)
+        nc.scalar.activation(s8, sh[:], ACT.Copy, scale=0.125)
+        nc.scalar.activation(s2, sh[:], ACT.Copy, scale=2.0)
+        nc.scalar.activation(og8, ogt[:], ACT.Copy, scale=0.125)
+        nc.scalar.activation(ss2, sh[:], ACT.Copy, scale=s2)
 
         def cast(grouped, raw):
             nc.scalar.copy(grouped[:], raw[:].rearrange("p t w -> p w t"))
@@ -112,7 +112,7 @@ def tile_attend_hvspreadpool_kernel(tc, tab_words, tab_scales, w1, share, wo, dy
         def direction_product(h, words):
             nc.tensor.matmul_mx(out=pt[h][:], lhsT=w1c[:].bitcast(FP8X4), lhsT_scale=w1s[:], rhs=words[:].bitcast(FP4X4), rhs_scale=gds[:, halves[h][0]], start=True, stop=True)
 
-        gdw0 = direction_half(0, sb.tile([P, J // 2], U16, name="gdw0", tag="w1_b", align_bytes=64))
+        gdw0 = direction_half(0, at(4864, "gdw0", [P, J // 2], U16))
         nc.vector.tensor_copy(gds[:], ds[:].indirect(offsets[:]))
         direction_product(0, gdw0)
 
@@ -133,6 +133,8 @@ def tile_attend_hvspreadpool_kernel(tc, tab_words, tab_scales, w1, share, wo, dy
         woc, wos = quant("wo", at(1792, "woc", [P, R], U32), wob)
         nc.vector.scalar_tensor_tensor(var[:], s2t[:], 0.125, msq[:], mult, sub)
         nc.scalar.activation(iv[:], var[:], ACT.Abs_reciprocal_sqrt, bias=0.05)
+        warm3 = t32("warm3", [P, 1])
+        nc.scalar.activation(warm3[:], iv[:, 0:1], ACT.Tanh)
         dyc, dys = quant("dy", at(2304, "dyc", [P, G], U32), dyb)
         direction_product(1, direction_half(1, at(1280, "gdw1", [P, J // 2], U16)))
         nc.tensor.matmul_mx(out=pc[:], lhsT=woc[:].bitcast(FP8X4), lhsT_scale=wos[:], rhs=dyc[:].bitcast(FP8X4), rhs_scale=dys[:], start=True, stop=True)

@@ -3,8 +3,10 @@ from contextlib import ExitStack
 import concourse.mybir as mybir
 
 K, R, F, T, J, G = 512, 128, 512, 2048, 512, 64
-W = J // G
+GROUP = J // G
 P = 128
+PACK = 4
+EPS = 0.05
 FLOPS = 2 * K * R * J * 2 + 2 * F * R * G
 
 F32 = mybir.dt.float32
@@ -19,185 +21,219 @@ ACT = mybir.ActivationFunctionType
 ALU = mybir.AluOpType
 AX = mybir.AxisListType
 
+ALIGN = 64
+AT_WO_BF16 = 0
+AT_SUM_A = AT_WO_BF16 + R * PACK * 2
+AT_DTAB_SCALES = AT_SUM_A - ALIGN
+AT_SUM_SQ = AT_SUM_A + G * 4
+AT_MEAN_SQ = AT_SUM_SQ + G * 4
+AT_WO_CODES = AT_MEAN_SQ + G * 4
+AT_DY_CODES = AT_WO_CODES + R * 4
+AT_DY_BF16 = AT_DY_CODES + G * 4
+AT_W1_RAW = AT_DY_BF16 + G * PACK * 2
+AT_TAB_SCALES = AT_W1_RAW + PACK * R * 4
+AT_DTAB_WORDS = (AT_TAB_SCALES - J // 2, AT_SUM_SQ)
+assert AT_DY_BF16 < AT_DTAB_SCALES + T <= AT_W1_RAW
+
 
 def tile_attend_hvspreadpool_kernel(tc, tab_words, tab_scales, w1, share, wo, dy, dtab_words, dtab_scales, og, base, offs, out):
     nc = tc.nc
     mult, add, sub = ALU.mult, ALU.add, ALU.subtract
     with ExitStack() as ctx:
         sb = ctx.enter_context(tc.tile_pool(name="sb", bufs=1))
-        shared = ctx.enter_context(tc.tile_pool(name="shared", bufs=1))
+        reused = ctx.enter_context(tc.tile_pool(name="reused", bufs=1))
         ps = ctx.enter_context(tc.psum_pool(name="ps", bufs=1))
 
-        def t32(name, shape, tag=None):
-            return sb.tile(shape, F32, name=name, tag=tag or name, align_bytes=64)
+        def own(name, shape, dtype=F32):
+            return sb.tile(shape, dtype, name=name, align_bytes=ALIGN)
 
-        def at(offset, name, shape, dtype=F32):
-            return shared.tile(shape, dtype, name=name, offset=offset, align_bytes=64)
+        def placed(offset, name, shape, dtype=F32):
+            return reused.tile(shape, dtype, name=name, offset=offset, align_bytes=ALIGN)
 
-        def grp(ap):
-            return ap.rearrange("p (g i) -> p g i", i=W)
+        def grouped(ap):
+            return ap.rearrange("p (g i) -> p g i", i=GROUP)
 
         def spread(ap):
-            return ap.unsqueeze(2).to_broadcast([P, ap.shape[1], W])
+            return ap.unsqueeze(2).to_broadcast([P, ap.shape[1], GROUP])
+
+        def twice(ap):
+            return ap.unsqueeze(1).to_broadcast([P, 2, G])
 
         offsets = sb.tile([P, J // 16], U16, name="offsets")
-        tw = sb.tile([P, T], U16, name="tw", align_bytes=64)
-        dw = sb.tile([P, T], U16, name="dw", align_bytes=64)
-        ts = at(5120, "ts", [P, T], U8)
-        ds = at(960, "ds", [P, T], U8)
-        w1r = at(3072, "w1r", [P, 4, R])
-        wor = t32("wor", [P, 4, R])
-        dyr = t32("dyr", [P, 4, G])
-        bs = t32("bs", [P, J])
-        sh = t32("sh", [P, 1])
-        ogt = t32("ogt", [P, 1])
-        warm = t32("warm", [P, 1])
-        warm2 = t32("warm2", [P, 1])
+        tab_w = own("tab_w", [P, T], U16)
+        dtab_w = own("dtab_w", [P, T], U16)
+        tab_s = placed(AT_TAB_SCALES, "tab_s", [P, T], U8)
+        dtab_s = placed(AT_DTAB_SCALES, "dtab_s", [P, T], U8)
+        w1_raw = placed(AT_W1_RAW, "w1_raw", [P, PACK, R])
+        wo_raw = own("wo_raw", [P, PACK, R])
+        dy_raw = own("dy_raw", [P, PACK, G])
+        base_sb = own("base_sb", [P, J])
+        share_sb = own("share_sb", [P, 1])
+        og_sb = own("og_sb", [P, 1])
 
-        nc.vector.memset(ts[:].bitcast(I32), 0)
-        nc.vector.memset(ds[:].bitcast(I32), 0)
-        nc.gpsimd.memset(warm[:], 1.0)
-        nc.scalar.dma_start(sh[:], share)
-        nc.scalar.dma_start(ogt[:], og)
-        nc.scalar.activation(warm2[:], warm[:], ACT.Abs_reciprocal_sqrt)
-        nc.sync.dma_start(offsets[:], offs)
-        def load_scales(tile, rows):
-            by_row = rows[0].rearrange("(q r) c -> r q c", r=4)
+        nc.vector.memset(tab_s[:].bitcast(I32), 0)
+        nc.vector.memset(dtab_s[:].bitcast(I32), 0)
+
+        warm_in = own("warm_in", [P, 1])
+        warm_root = own("warm_root", [P, 1])
+        nc.gpsimd.memset(warm_in[:], 1.0)
+        nc.scalar.activation(warm_root[:], warm_in[:], ACT.Abs_reciprocal_sqrt)
+
+        def load_scales(window, rows):
+            by_r = rows[0].rearrange("(q r) c -> r q c", r=4)
             for r in range(4):
-                nc.sync.dma_start(tile[r:P:32, :].bitcast(I32), by_row[r].bitcast(I32))
+                nc.sync.dma_start(window[r:P:32, :].bitcast(I32), by_r[r].bitcast(I32))
 
-        nc.sync.dma_start(tw[:].bitcast(I32), tab_words[0].bitcast(I32))
-        load_scales(ts, tab_scales)
-        nc.sync.dma_start(w1r[:], w1.rearrange("(p t) r -> p t r", t=4))
-        nc.sync.dma_start(dw[:].bitcast(I32), dtab_words[0].bitcast(I32))
-        load_scales(ds, dtab_scales)
-        nc.sync.dma_start(wor[:], wo.rearrange("(p t) r -> p t r", t=4))
-        nc.sync.dma_start(dyr[:], dy.rearrange("(p t) g -> p t g", t=4))
-        nc.sync.dma_start(bs[:], base)
+        nc.sync.dma_start(offsets[:], offs)
+        nc.sync.dma_start(tab_w[:].bitcast(I32), tab_words[0].bitcast(I32))
+        load_scales(tab_s, tab_scales)
+        nc.sync.dma_start(w1_raw[:], w1.rearrange("(p t) r -> p t r", t=PACK))
+        nc.sync.dma_start(dtab_w[:].bitcast(I32), dtab_words[0].bitcast(I32))
+        nc.sync.dma_start(share_sb[:], share)
+        nc.sync.dma_start(og_sb[:], og)
+        load_scales(dtab_s, dtab_scales)
+        nc.sync.dma_start(wo_raw[:], wo.rearrange("(p t) r -> p t r", t=PACK))
+        nc.sync.dma_start(dy_raw[:], dy.rearrange("(p t) g -> p t g", t=PACK))
+        nc.sync.dma_start(base_sb[:], base)
 
-        con = t32("con", [P, 4])
-        s8, s2, ss2, og8 = con[:, 0:1], con[:, 1:2], con[:, 2:3], con[:, 3:4]
-        nc.scalar.activation(s8, sh[:], ACT.Copy, scale=0.125)
-        nc.scalar.activation(s2, sh[:], ACT.Copy, scale=2.0)
-        nc.scalar.activation(og8, ogt[:], ACT.Copy, scale=0.125)
-        nc.scalar.activation(ss2, sh[:], ACT.Copy, scale=s2)
+        factors = own("factors", [P, 4])
+        s_8th, s_2x, ss_2x, og_8th = (factors[:, i : i + 1] for i in range(4))
+        nc.scalar.activation(s_8th, share_sb[:], ACT.Copy, scale=1.0 / GROUP)
+        nc.scalar.activation(s_2x, share_sb[:], ACT.Copy, scale=2.0)
+        nc.scalar.activation(og_8th, og_sb[:], ACT.Copy, scale=1.0 / GROUP)
+        nc.scalar.activation(ss_2x, share_sb[:], ACT.Copy, scale=s_2x)
 
-        def cast(grouped, raw):
-            nc.scalar.copy(grouped[:], raw[:].rearrange("p t w -> p w t"))
-            return grouped
+        def round_to_bf16(dst, raw):
+            nc.scalar.copy(dst[:], raw[:].rearrange("p t w -> p w t"))
+            return dst
 
-        def quant(name, codes, grouped):
-            scales = sb.tile([P, codes.shape[1]], U8, name=name + "_s", align_bytes=64)
-            nc.vector.quantize_mx(out=codes[:].bitcast(FP8X4), scales=scales[:], in_=grouped[:].rearrange("p w t -> p (w t)"))
-            return codes, scales
+        def quantise(name, codes, src):
+            scales = own(name, [P, codes.shape[1]], U8)
+            nc.vector.quantize_mx(out=codes[:].bitcast(FP8X4), scales=scales[:], in_=src[:].rearrange("p w t -> p (w t)"))
+            return codes[:].bitcast(FP8X4), scales[:]
 
-        halves = [(slice(0, J // 2), slice(0, G // 2)), (slice(J // 2, J), slice(G // 2, G))]
-        (c0, g0), (c1, g1) = halves
-        gtw = sb.tile([P, J], U16, name="gtw", align_bytes=64)
-        gts = sb.tile([P, J], U8, name="gts", align_bytes=64)
-        gds = sb.tile([P, J], U8, name="gds", align_bytes=64)
-        pa = ps.tile([P, J], F32, name="pa")
-        pt = [ps.tile([P, J // 2], F32, name="pt0"), ps.tile([P, J // 2], F32, name="pt1")]
-        pc = ps.tile([P, G], F32, name="pc")
+        def product(dst, lhs, rhs_words, rhs_scales):
+            nc.tensor.matmul_mx(out=dst[:], lhsT=lhs[0], lhsT_scale=lhs[1], rhs=rhs_words, rhs_scale=rhs_scales, start=True, stop=True)
 
-        nc.vector.tensor_copy(gtw[:], tw[:].indirect(offsets[:]))
-        nc.vector.tensor_copy(gts[:], ts[:].indirect(offsets[:]))
-        w1c, w1s = quant("w1", sb.tile([P, R], U32, name="w1c", align_bytes=64), cast(sb.tile([P, R, 4], BF16, name="w1_b", align_bytes=64), w1r))
-        nc.tensor.matmul_mx(out=pa[:], lhsT=w1c[:].bitcast(FP8X4), lhsT_scale=w1s[:], rhs=gtw[:].bitcast(FP4X4), rhs_scale=gts[:], start=True, stop=True)
+        slots = [slice(h * J // 2, (h + 1) * J // 2) for h in range(2)]
+        groups = [slice(h * G // 2, (h + 1) * G // 2) for h in range(2)]
+        a_ps = ps.tile([P, J], F32, name="a_ps")
+        ta_ps = [ps.tile([P, J // 2], F32, name="ta_ps%d" % h) for h in range(2)]
+        c0_ps = ps.tile([P, G], F32, name="c0_ps")
 
-        def direction_half(h, words):
-            nc.vector.tensor_copy(words[:], dw[:].indirect(offsets[:, 16 * h : 16 * (h + 1)]))
-            return words
+        tab_gw = own("tab_gw", [P, J], U16)
+        tab_gs = own("tab_gs", [P, J], U8)
+        nc.vector.tensor_copy(tab_gw[:], tab_w[:].indirect(offsets[:]))
+        nc.vector.tensor_copy(tab_gs[:], tab_s[:].indirect(offsets[:]))
+        w1_mx = quantise("w1_scales", own("w1_codes", [P, R], U32), round_to_bf16(own("w1_bf16", [P, R, PACK], BF16), w1_raw))
+        product(a_ps, w1_mx, tab_gw[:].bitcast(FP4X4), tab_gs[:])
 
-        def direction_product(h, words):
-            nc.tensor.matmul_mx(out=pt[h][:], lhsT=w1c[:].bitcast(FP8X4), lhsT_scale=w1s[:], rhs=words[:].bitcast(FP4X4), rhs_scale=gds[:, halves[h][0]], start=True, stop=True)
+        dtab_gs = own("dtab_gs", [P, J], U8)
 
-        gdw0 = direction_half(0, at(4864, "gdw0", [P, J // 2], U16))
-        nc.vector.tensor_copy(gds[:], ds[:].indirect(offsets[:]))
-        direction_product(0, gdw0)
+        def gather_dtab_words(h):
+            words = placed(AT_DTAB_WORDS[h], "dtab_gw%d" % h, [P, J // 2], U16)
+            nc.vector.tensor_copy(words[:], dtab_w[:].indirect(offsets[:, h * J // 32 : (h + 1) * J // 32]))
+            return words[:].bitcast(FP4X4)
 
-        sq = t32("sq", [P, J])
-        asb = t32("asb", [P, J])
-        s1 = at(1024, "s1", [P, G])
-        s2t = at(1280, "s2t", [P, G])
-        msq = at(1536, "msq", [P, G])
-        var = t32("var", [P, G])
-        iv = t32("iv", [P, G])
-        nc.scalar.copy(asb[:], pa[:])
-        nc.scalar.activation(sq[:], pa[:], ACT.Square)
-        nc.vector.tensor_reduce(s1[:], grp(asb[:]), AX.X, add)
-        nc.vector.tensor_reduce(s2t[:], grp(sq[:]), AX.X, add)
-        nc.vector.scalar_tensor_tensor(msq[:], s1[:], 1.0 / 64, s1[:], mult, mult)
-        wob = cast(at(0, "wob", [P, R, 4], BF16), wor)
-        dyb = cast(at(2560, "dyb", [P, G, 4], BF16), dyr)
-        woc, wos = quant("wo", at(1792, "woc", [P, R], U32), wob)
-        nc.vector.scalar_tensor_tensor(var[:], s2t[:], 0.125, msq[:], mult, sub)
-        nc.scalar.activation(iv[:], var[:], ACT.Abs_reciprocal_sqrt, bias=0.05)
-        warm3 = t32("warm3", [P, 1])
-        nc.scalar.activation(warm3[:], iv[:, 0:1], ACT.Tanh)
-        dyc, dys = quant("dy", at(2304, "dyc", [P, G], U32), dyb)
-        direction_product(1, direction_half(1, at(1280, "gdw1", [P, J // 2], U16)))
-        nc.tensor.matmul_mx(out=pc[:], lhsT=woc[:].bitcast(FP8X4), lhsT_scale=wos[:], rhs=dyc[:].bitcast(FP8X4), rhs_scale=dys[:], start=True, stop=True)
+        first_words = gather_dtab_words(0)
+        nc.vector.tensor_copy(dtab_gs[:], dtab_s[:].indirect(offsets[:]))
+        product(ta_ps[0], w1_mx, first_words, dtab_gs[:, slots[0]])
 
-        v = t32("v", [P, G])
-        pre = t32("pre", [P, G])
-        gg = t32("gg", [P, G])
-        u = t32("u", [P, G])
-        u2 = t32("u2", [P, G])
-        nc.vector.scalar_tensor_tensor(v[:], var[:], 0.05, iv[:], add, mult)
-        nc.vector.scalar_tensor_tensor(pre[:], s1[:], s8, v[:], mult, add)
-        nc.scalar.activation(u[:], pre[:], ACT.Tanh)
-        nc.scalar.activation(u2[:], u[:], ACT.Square)
+        a_sq = own("a_sq", [P, J])
+        a_sb = own("a_sb", [P, J])
+        sum_a = placed(AT_SUM_A, "sum_a", [P, G])
+        sum_sq = placed(AT_SUM_SQ, "sum_sq", [P, G])
+        mean_sq = placed(AT_MEAN_SQ, "mean_sq", [P, G])
+        var = own("var", [P, G])
+        iv = own("iv", [P, G])
+        nc.scalar.copy(a_sb[:], a_ps[:])
+        nc.scalar.activation(a_sq[:], a_ps[:], ACT.Square)
+        nc.vector.tensor_reduce(sum_a[:], grouped(a_sb[:]), AX.X, add)
+        nc.vector.tensor_reduce(sum_sq[:], grouped(a_sq[:]), AX.X, add)
+        nc.vector.scalar_tensor_tensor(mean_sq[:], sum_a[:], 1.0 / GROUP**2, sum_a[:], mult, mult)
+        wo_bf16 = round_to_bf16(placed(AT_WO_BF16, "wo_bf16", [P, R, PACK], BF16), wo_raw)
+        dy_bf16 = round_to_bf16(placed(AT_DY_BF16, "dy_bf16", [P, G, PACK], BF16), dy_raw)
+        wo_mx = quantise("wo_scales", placed(AT_WO_CODES, "wo_codes", [P, R], U32), wo_bf16)
+        nc.vector.scalar_tensor_tensor(var[:], sum_sq[:], 1.0 / GROUP, mean_sq[:], mult, sub)
+        nc.scalar.activation(iv[:], var[:], ACT.Abs_reciprocal_sqrt, bias=EPS)
+        warm_tanh = own("warm_tanh", [P, 1])
+        nc.scalar.activation(warm_tanh[:], iv[:, 0:1], ACT.Tanh)
+        dy_mx = quantise("dy_scales", placed(AT_DY_CODES, "dy_codes", [P, G], U32), dy_bf16)
+        product(ta_ps[1], w1_mx, gather_dtab_words(1), dtab_gs[:, slots[1]])
+        product(c0_ps, wo_mx, dy_mx[0], dy_mx[1])
 
-        prt = t32("prt", [P, J + G], tag="var")
-        pr, t1 = prt[:, 0:J], prt[:, J : J + G]
-        cr = t32("cr", [P, G])
-        cv = t32("cv", [P, G])
-        mt = t32("mt", [P, G])
-        nb = t32("nb", [P, G])
-        x = t32("x", [P, G])
-        xi = t32("xi", [P, G])
-        y = t32("y", [P, G])
-        co = t32("co", [P, 3, G])
-        for h, (cols, gs) in enumerate(halves):
-            nc.vector.scalar_tensor_tensor(pr[:, cols], pt[h][:], 0.125, asb[:, cols], mult, mult)
-            nc.vector.tensor_reduce(t1[:, gs], grp(pt[h][:]), AX.X, add)
-        nc.vector.scalar_tensor_tensor(gg[:], pc[:], og8, iv[:], mult, mult)
-        nc.vector.scalar_tensor_tensor(x[:], u[:], 2.0, iv[:], mult, add)
-        nc.vector.scalar_tensor_tensor(y[:], u[:], ss2, v[:], mult, mult)
-        nc.vector.scalar_tensor_tensor(nb[:], u2[:], 1.0, gg[:], sub, mult)
-        nc.vector.scalar_tensor_tensor(mt[:], s1[:], 1.0 / 64, t1, mult, mult)
-        nc.vector.tensor_tensor(xi[:], x[:], iv[:], mult)
-        nc.vector.tensor_reduce(cr[:], grp(pr), AX.X, add)
-        nc.vector.scalar_tensor_tensor(co[:, 2, :], y[:], 1.0, nb[:], add, mult)
-        nc.vector.scalar_tensor_tensor(co[:, 1, :], u[:], s2, nb[:], mult, mult)
-        nc.vector.tensor_tensor(co[:, 0, :], xi[:], nb[:], mult)
-        nc.vector.tensor_tensor(cv[:], cr[:], mt[:], sub)
+        v = own("v", [P, G])
+        arg = own("arg", [P, G])
+        u = own("u", [P, G])
+        u_sq = own("u_sq", [P, G])
+        nc.vector.scalar_tensor_tensor(v[:], var[:], EPS, iv[:], add, mult)
+        nc.vector.scalar_tensor_tensor(arg[:], sum_a[:], s_8th, v[:], mult, add)
+        nc.scalar.activation(u[:], arg[:], ACT.Tanh)
+        nc.scalar.activation(u_sq[:], u[:], ACT.Square)
 
-        bta = t32("bta", [P, J])
-        yb = t32("yb", [P, J])
-        ad0 = t32("ad0", [P, 2, G])
-        ad1 = t32("ad1", [P, 2, G])
-        ad = t32("ad", [P, 2, G])
-        am = t32("am", [P, G])
-        cc = t32("cc", [P, G])
-        e1 = t32("e1", [P, J])
-        e2 = t32("e2", [P, J])
-        res = [t32("res0", [P, J // 2]), t32("res1", [P, J // 2])]
-        nc.vector.scalar_tensor_tensor(ad0[:], t1.unsqueeze(1).to_broadcast([P, 2, G]), 0.125, co[:, 1:3, :], mult, mult)
-        nc.vector.tensor_tensor(grp(bta[:, c0]), grp(pt[0][:]), spread(nb[:, g0]), mult)
-        nc.vector.tensor_tensor(ad1[:], cv[:].unsqueeze(1).to_broadcast([P, 2, G]), co[:, 0:2, :], mult)
-        nc.vector.tensor_tensor(grp(bta[:, c1]), grp(pt[1][:]), spread(nb[:, g1]), mult)
-        nc.vector.tensor_tensor(ad[:], ad0[:], ad1[:], add)
-        nc.vector.tensor_tensor(yb[:, c0], bs[:, c0], bta[:, c0], sub)
-        nc.vector.scalar_tensor_tensor(am[:], s1[:], 0.125, ad[:, 0, :], mult, mult)
-        nc.vector.tensor_tensor(grp(e1[:, c0]), grp(asb[:, c0]), spread(ad[:, 0, g0]), mult)
-        nc.vector.tensor_tensor(cc[:], ad[:, 1, :], am[:], sub)
-        nc.vector.tensor_tensor(yb[:, c1], bs[:, c1], bta[:, c1], sub)
-        nc.vector.tensor_tensor(grp(e2[:, c0]), grp(yb[:, c0]), spread(cc[:, g0]), add)
-        nc.vector.tensor_tensor(grp(e1[:, c1]), grp(asb[:, c1]), spread(ad[:, 0, g1]), mult)
-        nc.vector.tensor_tensor(grp(e2[:, c1]), grp(yb[:, c1]), spread(cc[:, g1]), add)
-        nc.vector.tensor_tensor(res[0][:], e1[:, c0], e2[:, c0], add)
-        nc.sync.dma_start(out[:, c0], res[0][:])
-        nc.vector.tensor_tensor(res[1][:], e1[:, c1], e2[:, c1], add)
-        nc.sync.dma_start(out[:, c1], res[1][:])
+        ta_work = sb.tile([P, J + G], F32, name="ta_work", tag="var", align_bytes=ALIGN)
+        ta_a, sum_ta = ta_work[:, 0:J], ta_work[:, J : J + G]
+        for h in range(2):
+            nc.vector.scalar_tensor_tensor(ta_a[:, slots[h]], ta_ps[h][:], 1.0 / GROUP, a_sb[:, slots[h]], mult, mult)
+            nc.vector.tensor_reduce(sum_ta[:, groups[h]], grouped(ta_ps[h][:]), AX.X, add)
+
+        gain = own("gain", [P, G])
+        iv_2u = own("iv_2u", [P, G])
+        ssuv = own("ssuv", [P, G])
+        nb = own("nb", [P, G])
+        m_xm = own("m_xm", [P, G])
+        curve = own("curve", [P, G])
+        mean_ta_a = own("mean_ta_a", [P, G])
+        cov = own("cov", [P, G])
+        fac = own("fac", [P, 3, G])
+        nc.vector.scalar_tensor_tensor(gain[:], c0_ps[:], og_8th, iv[:], mult, mult)
+        nc.vector.scalar_tensor_tensor(iv_2u[:], u[:], 2.0, iv[:], mult, add)
+        nc.vector.scalar_tensor_tensor(ssuv[:], u[:], ss_2x, v[:], mult, mult)
+        nc.vector.scalar_tensor_tensor(nb[:], u_sq[:], 1.0, gain[:], sub, mult)
+        nc.vector.scalar_tensor_tensor(m_xm[:], sum_a[:], 1.0 / GROUP**2, sum_ta, mult, mult)
+        nc.vector.tensor_tensor(curve[:], iv_2u[:], iv[:], mult)
+        nc.vector.tensor_reduce(mean_ta_a[:], grouped(ta_a), AX.X, add)
+        nc.vector.scalar_tensor_tensor(fac[:, 2, :], ssuv[:], 1.0, nb[:], add, mult)
+        nc.vector.scalar_tensor_tensor(fac[:, 1, :], u[:], s_2x, nb[:], mult, mult)
+        nc.vector.tensor_tensor(fac[:, 0, :], curve[:], nb[:], mult)
+        nc.vector.tensor_tensor(cov[:], mean_ta_a[:], m_xm[:], sub)
+
+        from_xm = own("from_xm", [P, 2, G])
+        from_cov = own("from_cov", [P, 2, G])
+        ca_cd = own("ca_cd", [P, 2, G])
+        ca_m = own("ca_m", [P, G])
+        shift = own("shift", [P, G])
+        nb_ta = own("nb_ta", [P, J])
+        based = own("based", [P, J])
+        ca_a = own("ca_a", [P, J])
+        shifted = own("shifted", [P, J])
+        result = [own("result%d" % h, [P, J // 2]) for h in range(2)]
+
+        def times_nb(h):
+            nc.vector.tensor_tensor(grouped(nb_ta[:, slots[h]]), grouped(ta_ps[h][:]), spread(nb[:, groups[h]]), mult)
+
+        def from_base(h):
+            nc.vector.tensor_tensor(based[:, slots[h]], base_sb[:, slots[h]], nb_ta[:, slots[h]], sub)
+
+        def times_ca(h):
+            nc.vector.tensor_tensor(grouped(ca_a[:, slots[h]]), grouped(a_sb[:, slots[h]]), spread(ca_cd[:, 0, groups[h]]), mult)
+
+        def plus_shift(h):
+            nc.vector.tensor_tensor(grouped(shifted[:, slots[h]]), grouped(based[:, slots[h]]), spread(shift[:, groups[h]]), add)
+
+        nc.vector.scalar_tensor_tensor(from_xm[:], twice(sum_ta), 1.0 / GROUP, fac[:, 1:3, :], mult, mult)
+        times_nb(0)
+        nc.vector.tensor_tensor(from_cov[:], twice(cov[:]), fac[:, 0:2, :], mult)
+        times_nb(1)
+        nc.vector.tensor_tensor(ca_cd[:], from_xm[:], from_cov[:], add)
+        from_base(0)
+        nc.vector.scalar_tensor_tensor(ca_m[:], sum_a[:], 1.0 / GROUP, ca_cd[:, 0, :], mult, mult)
+        times_ca(0)
+        nc.vector.tensor_tensor(shift[:], ca_cd[:, 1, :], ca_m[:], sub)
+        from_base(1)
+        plus_shift(0)
+        times_ca(1)
+        plus_shift(1)
+        for h in range(2):
+            nc.vector.tensor_tensor(result[h][:], ca_a[:, slots[h]], shifted[:, slots[h]], add)
+            nc.sync.dma_start(out[:, slots[h]], result[h][:])

from contextlib import ExitStack

import concourse.mybir as mybir

K, R, F, T, J, G = 512, 128, 512, 2048, 512, 64
GROUP = J // G
P = 128
PACK = 4
EPS = 0.05
FLOPS = 2 * K * R * J * 2 + 2 * F * R * G

F32 = mybir.dt.float32
BF16 = mybir.dt.bfloat16
I32 = mybir.dt.int32
U32 = mybir.dt.uint32
U16 = mybir.dt.uint16
U8 = mybir.dt.uint8
FP8X4 = mybir.dt.float8_e4m3fn_x4
FP4X4 = mybir.dt.float4_e2m1fn_x4
ACT = mybir.ActivationFunctionType
ALU = mybir.AluOpType
AX = mybir.AxisListType

ALIGN = 64
AT_WO_BF16 = 0
AT_SUM_A = AT_WO_BF16 + R * PACK * 2
AT_DTAB_SCALES = AT_SUM_A - ALIGN
AT_SUM_SQ = AT_SUM_A + G * 4
AT_MEAN_SQ = AT_SUM_SQ + G * 4
AT_WO_CODES = AT_MEAN_SQ + G * 4
AT_DY_CODES = AT_WO_CODES + R * 4
AT_DY_BF16 = AT_DY_CODES + G * 4
AT_W1_RAW = AT_DY_BF16 + G * PACK * 2
AT_TAB_SCALES = AT_W1_RAW + PACK * R * 4
AT_DTAB_WORDS = (AT_TAB_SCALES - J // 2, AT_SUM_SQ)
assert AT_DY_BF16 < AT_DTAB_SCALES + T <= AT_W1_RAW


def tile_attend_hvspreadpool_kernel(tc, tab_words, tab_scales, w1, share, wo, dy, dtab_words, dtab_scales, og, base, offs, out):
    nc = tc.nc
    mult, add, sub = ALU.mult, ALU.add, ALU.subtract
    with ExitStack() as ctx:
        sb = ctx.enter_context(tc.tile_pool(name="sb", bufs=1))
        reused = ctx.enter_context(tc.tile_pool(name="reused", bufs=1))
        ps = ctx.enter_context(tc.psum_pool(name="ps", bufs=1))

        def own(name, shape, dtype=F32):
            return sb.tile(shape, dtype, name=name, align_bytes=ALIGN)

        def placed(offset, name, shape, dtype=F32):
            return reused.tile(shape, dtype, name=name, offset=offset, align_bytes=ALIGN)

        def grouped(ap):
            return ap.rearrange("p (g i) -> p g i", i=GROUP)

        def spread(ap):
            return ap.unsqueeze(2).to_broadcast([P, ap.shape[1], GROUP])

        def twice(ap):
            return ap.unsqueeze(1).to_broadcast([P, 2, G])

        offsets = sb.tile([P, J // 16], U16, name="offsets")
        tab_w = own("tab_w", [P, T], U16)
        dtab_w = own("dtab_w", [P, T], U16)
        tab_s = placed(AT_TAB_SCALES, "tab_s", [P, T], U8)
        dtab_s = placed(AT_DTAB_SCALES, "dtab_s", [P, T], U8)
        w1_raw = placed(AT_W1_RAW, "w1_raw", [P, PACK, R])
        wo_raw = own("wo_raw", [P, PACK, R])
        dy_raw = own("dy_raw", [P, PACK, G])
        base_sb = own("base_sb", [P, J])
        share_sb = own("share_sb", [P, 1])
        og_sb = own("og_sb", [P, 1])

        nc.vector.memset(tab_s[:].bitcast(I32), 0)
        nc.vector.memset(dtab_s[:].bitcast(I32), 0)

        warm_in = own("warm_in", [P, 1])
        warm_root = own("warm_root", [P, 1])
        nc.gpsimd.memset(warm_in[:], 1.0)
        nc.scalar.activation(warm_root[:], warm_in[:], ACT.Abs_reciprocal_sqrt)

        def load_scales(window, rows):
            by_r = rows[0].rearrange("(q r) c -> r q c", r=4)
            for r in range(4):
                nc.sync.dma_start(window[r:P:32, :].bitcast(I32), by_r[r].bitcast(I32))

        nc.sync.dma_start(offsets[:], offs)
        nc.sync.dma_start(tab_w[:].bitcast(I32), tab_words[0].bitcast(I32))
        load_scales(tab_s, tab_scales)
        nc.sync.dma_start(w1_raw[:], w1.rearrange("(p t) r -> p t r", t=PACK))
        nc.sync.dma_start(dtab_w[:].bitcast(I32), dtab_words[0].bitcast(I32))
        nc.sync.dma_start(share_sb[:], share)
        nc.sync.dma_start(og_sb[:], og)
        load_scales(dtab_s, dtab_scales)
        nc.sync.dma_start(wo_raw[:], wo.rearrange("(p t) r -> p t r", t=PACK))
        nc.sync.dma_start(dy_raw[:], dy.rearrange("(p t) g -> p t g", t=PACK))
        nc.sync.dma_start(base_sb[:], base)

        factors = own("factors", [P, 4])
        s_8th, s_2x, ss_2x, og_8th = (factors[:, i : i + 1] for i in range(4))
        nc.scalar.activation(s_8th, share_sb[:], ACT.Copy, scale=1.0 / GROUP)
        nc.scalar.activation(s_2x, share_sb[:], ACT.Copy, scale=2.0)
        nc.scalar.activation(og_8th, og_sb[:], ACT.Copy, scale=1.0 / GROUP)
        nc.scalar.activation(ss_2x, share_sb[:], ACT.Copy, scale=s_2x)

        def round_to_bf16(dst, raw):
            nc.scalar.copy(dst[:], raw[:].rearrange("p t w -> p w t"))
            return dst

        def quantise(name, codes, src):
            scales = own(name, [P, codes.shape[1]], U8)
            nc.vector.quantize_mx(out=codes[:].bitcast(FP8X4), scales=scales[:], in_=src[:].rearrange("p w t -> p (w t)"))
            return codes[:].bitcast(FP8X4), scales[:]

        def product(dst, lhs, rhs_words, rhs_scales):
            nc.tensor.matmul_mx(out=dst[:], lhsT=lhs[0], lhsT_scale=lhs[1], rhs=rhs_words, rhs_scale=rhs_scales, start=True, stop=True)

        slots = [slice(h * J // 2, (h + 1) * J // 2) for h in range(2)]
        groups = [slice(h * G // 2, (h + 1) * G // 2) for h in range(2)]
        a_ps = ps.tile([P, J], F32, name="a_ps")
        ta_ps = [ps.tile([P, J // 2], F32, name="ta_ps%d" % h) for h in range(2)]
        c0_ps = ps.tile([P, G], F32, name="c0_ps")

        tab_gw = own("tab_gw", [P, J], U16)
        tab_gs = own("tab_gs", [P, J], U8)
        nc.vector.tensor_copy(tab_gw[:], tab_w[:].indirect(offsets[:]))
        nc.vector.tensor_copy(tab_gs[:], tab_s[:].indirect(offsets[:]))
        w1_mx = quantise("w1_scales", own("w1_codes", [P, R], U32), round_to_bf16(own("w1_bf16", [P, R, PACK], BF16), w1_raw))
        product(a_ps, w1_mx, tab_gw[:].bitcast(FP4X4), tab_gs[:])

        dtab_gs = own("dtab_gs", [P, J], U8)

        def gather_dtab_words(h):
            words = placed(AT_DTAB_WORDS[h], "dtab_gw%d" % h, [P, J // 2], U16)
            nc.vector.tensor_copy(words[:], dtab_w[:].indirect(offsets[:, h * J // 32 : (h + 1) * J // 32]))
            return words[:].bitcast(FP4X4)

        first_words = gather_dtab_words(0)
        nc.vector.tensor_copy(dtab_gs[:], dtab_s[:].indirect(offsets[:]))
        product(ta_ps[0], w1_mx, first_words, dtab_gs[:, slots[0]])

        a_sq = own("a_sq", [P, J])
        a_sb = own("a_sb", [P, J])
        sum_a = placed(AT_SUM_A, "sum_a", [P, G])
        sum_sq = placed(AT_SUM_SQ, "sum_sq", [P, G])
        mean_sq = placed(AT_MEAN_SQ, "mean_sq", [P, G])
        var = own("var", [P, G])
        iv = own("iv", [P, G])
        nc.scalar.copy(a_sb[:], a_ps[:])
        nc.scalar.activation(a_sq[:], a_ps[:], ACT.Square)
        nc.vector.tensor_reduce(sum_a[:], grouped(a_sb[:]), AX.X, add)
        nc.vector.tensor_reduce(sum_sq[:], grouped(a_sq[:]), AX.X, add)
        nc.vector.scalar_tensor_tensor(mean_sq[:], sum_a[:], 1.0 / GROUP**2, sum_a[:], mult, mult)
        wo_bf16 = round_to_bf16(placed(AT_WO_BF16, "wo_bf16", [P, R, PACK], BF16), wo_raw)
        dy_bf16 = round_to_bf16(placed(AT_DY_BF16, "dy_bf16", [P, G, PACK], BF16), dy_raw)
        wo_mx = quantise("wo_scales", placed(AT_WO_CODES, "wo_codes", [P, R], U32), wo_bf16)
        nc.vector.scalar_tensor_tensor(var[:], sum_sq[:], 1.0 / GROUP, mean_sq[:], mult, sub)
        nc.scalar.activation(iv[:], var[:], ACT.Abs_reciprocal_sqrt, bias=EPS)
        warm_tanh = own("warm_tanh", [P, 1])
        nc.scalar.activation(warm_tanh[:], iv[:, 0:1], ACT.Tanh)
        dy_mx = quantise("dy_scales", placed(AT_DY_CODES, "dy_codes", [P, G], U32), dy_bf16)
        product(ta_ps[1], w1_mx, gather_dtab_words(1), dtab_gs[:, slots[1]])
        product(c0_ps, wo_mx, dy_mx[0], dy_mx[1])

        v = own("v", [P, G])
        arg = own("arg", [P, G])
        u = own("u", [P, G])
        u_sq = own("u_sq", [P, G])
        nc.vector.scalar_tensor_tensor(v[:], var[:], EPS, iv[:], add, mult)
        nc.vector.scalar_tensor_tensor(arg[:], sum_a[:], s_8th, v[:], mult, add)
        nc.scalar.activation(u[:], arg[:], ACT.Tanh)
        nc.scalar.activation(u_sq[:], u[:], ACT.Square)

        ta_work = sb.tile([P, J + G], F32, name="ta_work", tag="var", align_bytes=ALIGN)
        ta_a, sum_ta = ta_work[:, 0:J], ta_work[:, J : J + G]
        for h in range(2):
            nc.vector.scalar_tensor_tensor(ta_a[:, slots[h]], ta_ps[h][:], 1.0 / GROUP, a_sb[:, slots[h]], mult, mult)
            nc.vector.tensor_reduce(sum_ta[:, groups[h]], grouped(ta_ps[h][:]), AX.X, add)

        gain = own("gain", [P, G])
        iv_2u = own("iv_2u", [P, G])
        ssuv = own("ssuv", [P, G])
        nb = own("nb", [P, G])
        m_xm = own("m_xm", [P, G])
        curve = own("curve", [P, G])
        mean_ta_a = own("mean_ta_a", [P, G])
        cov = own("cov", [P, G])
        fac = own("fac", [P, 3, G])
        nc.vector.scalar_tensor_tensor(gain[:], c0_ps[:], og_8th, iv[:], mult, mult)
        nc.vector.scalar_tensor_tensor(iv_2u[:], u[:], 2.0, iv[:], mult, add)
        nc.vector.scalar_tensor_tensor(ssuv[:], u[:], ss_2x, v[:], mult, mult)
        nc.vector.scalar_tensor_tensor(nb[:], u_sq[:], 1.0, gain[:], sub, mult)
        nc.vector.scalar_tensor_tensor(m_xm[:], sum_a[:], 1.0 / GROUP**2, sum_ta, mult, mult)
        nc.vector.tensor_tensor(curve[:], iv_2u[:], iv[:], mult)
        nc.vector.tensor_reduce(mean_ta_a[:], grouped(ta_a), AX.X, add)
        nc.vector.scalar_tensor_tensor(fac[:, 2, :], ssuv[:], 1.0, nb[:], add, mult)
        nc.vector.scalar_tensor_tensor(fac[:, 1, :], u[:], s_2x, nb[:], mult, mult)
        nc.vector.tensor_tensor(fac[:, 0, :], curve[:], nb[:], mult)
        nc.vector.tensor_tensor(cov[:], mean_ta_a[:], m_xm[:], sub)

        from_xm = own("from_xm", [P, 2, G])
        from_cov = own("from_cov", [P, 2, G])
        ca_cd = own("ca_cd", [P, 2, G])
        ca_m = own("ca_m", [P, G])
        shift = own("shift", [P, G])
        nb_ta = own("nb_ta", [P, J])
        based = own("based", [P, J])
        ca_a = own("ca_a", [P, J])
        shifted = own("shifted", [P, J])
        result = [own("result%d" % h, [P, J // 2]) for h in range(2)]

        def times_nb(h):
            nc.vector.tensor_tensor(grouped(nb_ta[:, slots[h]]), grouped(ta_ps[h][:]), spread(nb[:, groups[h]]), mult)

        def from_base(h):
            nc.vector.tensor_tensor(based[:, slots[h]], base_sb[:, slots[h]], nb_ta[:, slots[h]], sub)

        def times_ca(h):
            nc.vector.tensor_tensor(grouped(ca_a[:, slots[h]]), grouped(a_sb[:, slots[h]]), spread(ca_cd[:, 0, groups[h]]), mult)

        def plus_shift(h):
            nc.vector.tensor_tensor(grouped(shifted[:, slots[h]]), grouped(based[:, slots[h]]), spread(shift[:, groups[h]]), add)

        nc.vector.scalar_tensor_tensor(from_xm[:], twice(sum_ta), 1.0 / GROUP, fac[:, 1:3, :], mult, mult)
        times_nb(0)
        nc.vector.tensor_tensor(from_cov[:], twice(cov[:]), fac[:, 0:2, :], mult)
        times_nb(1)
        nc.vector.tensor_tensor(ca_cd[:], from_xm[:], from_cov[:], add)
        from_base(0)
        nc.vector.scalar_tensor_tensor(ca_m[:], sum_a[:], 1.0 / GROUP, ca_cd[:, 0, :], mult, mult)
        times_ca(0)
        nc.vector.tensor_tensor(shift[:], ca_cd[:, 1, :], ca_m[:], sub)
        from_base(1)
        plus_shift(0)
        times_ca(1)
        plus_shift(1)
        for h in range(2):
            nc.vector.tensor_tensor(result[h][:], ca_a[:, slots[h]], shifted[:, slots[h]], add)
            nc.sync.dma_start(out[:, slots[h]], result[h][:])
